import numpy as np
import ml_dtypes


def mxq(x, axis, fmt="e4m3"):
    dtype, down = {"e4m3": (ml_dtypes.float8_e4m3fn, 7), "e5m2": (ml_dtypes.float8_e5m2, 14)}[fmt]
    v = np.moveaxis(np.asarray(x, np.float32).astype(ml_dtypes.bfloat16).astype(np.float64), axis, -1)
    blocks = v.reshape(v.shape[:-1] + (-1, 32))
    amax = np.abs(blocks).max(-1, keepdims=True)
    byte = np.maximum(np.where(amax > 0, np.frexp(amax)[1] - 1 + 127, 0) - down, 1)
    scale = np.exp2(byte - 127.0)
    codes = (blocks / scale).astype(np.float32).astype(dtype).astype(np.float64)
    return np.moveaxis((codes * scale).reshape(v.shape), -1, axis)


WIDE = False


def mx_kscale(k):
    if not WIDE:
        return np.ones(k)
    levels = np.array([10, -10, 5, -5, 0])
    if k % 512:
        return np.exp2(np.random.permutation(np.resize(levels, k // 32))).repeat(32)
    a = np.empty((k // 512, 16))
    for p in range(k // 512):
        a[p, :8] = np.random.permutation(np.resize(levels, 8))
        for g in range(8):
            far = levels[np.abs(levels - a[p, g]) >= 10]
            a[p, g + 8] = far[np.random.randint(len(far))]
    return np.exp2(a.ravel()).repeat(32)


def f64(x):
    return np.asarray(x).astype(np.float64)


def striped(idx):
    return np.tile(np.asarray(idx).reshape(-1, 16).T, (8, 1)).astype(np.uint16)


def unstriped(offs):
    return offs[:16].T.reshape(-1).astype(np.int64)


E2M1 = np.array([0.0, 0.5, 1.0, 1.5, 2.0, 3.0, 4.0, 6.0, -0.0, -0.5, -1.0, -1.5, -2.0, -3.0, -4.0, -6.0])


def pack_weight(w, fmt):
    k, n = w.shape
    w = f64(np.asarray(w, np.float32).astype(ml_dtypes.bfloat16)).reshape(k // 32, 32, n)
    amax = np.abs(w).max(1)
    if fmt == "e4m3":
        byte = np.frexp(amax)[1] - 1 + 127 - 7
    else:
        mant, ex = np.frexp(amax / 6.0)
        byte = np.where(mant > 0.5, ex, ex - 1) + 127
    byte = np.clip(np.where(amax > 0, byte, 1), 1, 254)
    scaled = (w * np.exp2(127.0 - byte)[:, None, :]).reshape(k, n).astype(np.float32)
    by_word = np.ascontiguousarray(scaled.reshape(k // 512, 128, 4, n).transpose(0, 1, 3, 2))
    if fmt == "e4m3":
        words = by_word.astype(ml_dtypes.float8_e4m3fn).view(np.uint8)
    else:
        c = by_word.astype(ml_dtypes.float4_e2m1fn).view(np.uint8) & 0xF
        words = (c[..., 0::2] | (c[..., 1::2] << 4)).reshape(k // 512, 128, 2 * n)
    return np.ascontiguousarray(words), np.ascontiguousarray(byte.astype(np.uint8).reshape(k // 512, 16, n))


def unpack_weight(words, scales, fmt):
    g, _, n = scales.shape
    words = np.ascontiguousarray(words).reshape(g, 128, n, -1)
    if fmt == "e4m3":
        vals = words.view(ml_dtypes.float8_e4m3fn).astype(np.float64)
    else:
        nib = np.empty((g, 128, n, 4), np.uint8)
        nib[..., 0::2] = words & 0xF
        nib[..., 1::2] = words >> 4
        vals = E2M1[nib]
    vals = vals * np.repeat(np.exp2(scales.astype(np.float64) - 127.0), 8, axis=1)[..., None]
    return vals.transpose(0, 1, 3, 2).reshape(g * 512, n)


def bf(x):
    return np.asarray(x, np.float32).astype(ml_dtypes.bfloat16)


def planes(Y):
    r, m = Y.shape
    b = f64(bf(Y)).reshape(r // 32, 32, m)
    amax = np.abs(b).max(1)
    byte = np.clip(np.where(amax > 0, np.frexp(amax)[1] - 1 + 127 - 7, 1), 1, 254)
    codes = (b * np.exp2(127.0 - byte)[:, None, :]).reshape(r, m).astype(np.float32).astype(ml_dtypes.float8_e4m3fn).view(np.uint8)
    words = codes.reshape(r // 512, 128, 4, m).transpose(0, 1, 3, 2)
    return np.ascontiguousarray(words), np.ascontiguousarray(byte.astype(np.uint8).reshape(r // 512, 16, m))


K, T, J, N = 1024, 2048, 512, 512


def setup_inputs():
    n = np.random.standard_normal
    idx = np.random.permutation(T)[:J]
    fk = mx_kscale(K)
    wap = pack_weight(n((K, N)) * 1 / np.sqrt(K) * fk[:, None], "e2m1")
    wbp = pack_weight(n((K, N)) * 1 / np.sqrt(K) * fk[:, None], "e4m3")
    return {
        "xt": (n((K, T)) * np.random.uniform(0.3, 1.7, (1, T)) / fk[:, None]).astype(np.float32),
        "wa_words": wap[0],
        "wa_scales": wap[1],
        "wb_words": wbp[0],
        "wb_scales": wbp[1],
        "lm": (np.random.uniform(0.4, 1.4, (J, 1))).astype(np.float32),
        "offs": striped(idx),
    }


def reference(xt, wa_words, wa_scales, wb_words, wb_scales, lm, offs):
    idx = unstriped(offs)
    wau = unpack_weight(wa_words, wa_scales, "e2m1")
    wbu = unpack_weight(wb_words, wb_scales, "e4m3")
    xtidxq = mxq(f64(xt)[:, idx], 0, "e4m3")
    a = xtidxq.T @ wau
    b = xtidxq.T @ wbu
    sa = np.minimum(f64(lm) / np.sqrt(np.mean(np.square(a), axis=1, keepdims=True) + 0.01), 1.0)
    sb = np.minimum(f64(lm) / np.sqrt(np.mean(np.square(b), axis=1, keepdims=True) + 0.01), 1.0)
    y = a * sa + 0.5 * b * sb
    words, scales = planes(y)
    return y, words, scales

@@ -1,0 +1,226 @@
+from contextlib import ExitStack
+
+import concourse.mybir as mybir
+
+K, T, J, N = 1024, 2048, 512, 512
+FLOPS = 2 * 2 * J * K * N
+
+F32 = mybir.dt.float32
+BF16 = mybir.dt.bfloat16
+I32 = mybir.dt.int32
+U32 = mybir.dt.uint32
+U16 = mybir.dt.uint16
+U8 = mybir.dt.uint8
+FP8X4 = mybir.dt.float8_e4m3fn_x4
+FP4X4 = mybir.dt.float4_e2m1fn_x4
+ALU = mybir.AluOpType
+ACT = mybir.ActivationFunctionType
+
+P = 128
+PACK = 4
+PASSES = K // (P * PACK)
+QUADS = 4
+EPS = 0.01
+TINY = 1e-15
+HUGE = 1e15
+HALF = N // 2
+
+
+def tile_moe_expert_rows_held_to_size_pl_kernel(tc, xt, wa_words, wa_scales, wb_words, wb_scales, lm, offs, out_0, out_1, out_2):
+    nc = tc.nc
+    with ExitStack() as ctx:
+        keep = ctx.enter_context(tc.tile_pool(name="keep", bufs=1))
+        psum = ctx.enter_context(tc.psum_pool(name="psum", bufs=1))
+
+        offsets = keep.tile([P, J // 16], U16, name="offsets")
+        limit = keep.tile([P, PACK], F32, name="limit")
+        rows = [[keep.tile([P, T], F32, name="rows%d%d" % (g, r)) for r in range(PACK)] for g in range(PASSES)]
+        wa_codes = [keep.tile([P, 2 * N], U8, name="wa_codes%d" % g, align_bytes=64) for g in range(PASSES)]
+        wb_codes = [keep.tile([P, N], U32, name="wb_codes%d" % g, align_bytes=64) for g in range(PASSES)]
+        wa_sc = keep.tile([P, PASSES * N], U8, name="wa_sc", align_bytes=64)
+        wb_sc = keep.tile([P, PASSES * N], U8, name="wb_sc", align_bytes=64)
+        picked = [keep.tile([P, PACK, P, PACK], BF16, name="picked%d" % g, align_bytes=64) for g in range(PASSES)]
+        x_codes = [keep.tile([P, J], U32, name="x_codes%d" % g, align_bytes=64) for g in range(PASSES)]
+        x_sc = [keep.tile([P, J], U8, name="x_sc%d" % g, align_bytes=64) for g in range(PASSES)]
+        acc_a = [psum.tile([P, N], F32, name="acc_a%d" % t) for t in range(PACK)]
+        acc_b = [psum.tile([P, N], F32, name="acc_b%d" % t) for t in range(PACK)]
+        y = keep.tile([P, PACK, N], F32, name="y")
+        half_b = keep.tile([P, PACK, N], F32, name="half_b")
+        y_bf = [keep.tile([P, HALF, PACK], BF16, name="y_bf%d" % h, align_bytes=64) for h in range(2)]
+        y_codes = keep.tile([P, N], U32, name="y_codes", align_bytes=64)
+        y_sc = keep.tile([P, N], U8, name="y_sc", align_bytes=64)
+        mean_sq = keep.tile([P, PACK, 2], F32, name="mean_sq")
+        inv_rms = keep.tile([P, PACK, 2], F32, name="inv_rms")
+        factor = keep.tile([P, PACK, 2], F32, name="factor")
+        gain = keep.tile([P, PACK, 2], F32, name="gain")
+        bound_sq = keep.tile([P, PACK], F32, name="bound_sq")
+        bounded = keep.tile([P, PACK], F32, name="bounded")
+        inv_limit = keep.tile([P, PACK], F32, name="inv_limit")
+        stats = keep.tile([P, PACK, 16], F32, name="stats")
+        terms = keep.tile([P, PACK, 2, 2], F32, name="terms")
+        nc.vector.memset(stats[:, :, 6:10], 2.0 / N)
+
+        nc.vector.memset(wa_sc[:].bitcast(I32), 0)
+        nc.vector.memset(wb_sc[:].bitcast(I32), 0)
+
+        x_rows = xt.rearrange("(g p r) t -> g r p t", p=P, r=PACK)
+
+        def load_rows(g, r):
+            nc.sync.dma_start(out=rows[g][r][:], in_=x_rows[g, r])
+
+        def load_scales(plane, src, q):
+            nc.sync.dma_start(
+                out=plane[32 * q : 32 * q + 4, :].bitcast(I32).rearrange("r (g c) -> r g c", g=PASSES),
+                in_=src.bitcast(I32)[:, 4 * q : 4 * q + 4, :].rearrange("g r c -> r g c"),
+            )
+
+        def load_a(g):
+            nc.sync.dma_start(out=wa_codes[g][:].bitcast(I32), in_=wa_words[g].bitcast(I32))
+
+        def load_b(g):
+            nc.sync.dma_start(out=wb_codes[g][:].bitcast(I32), in_=wb_words[g].rearrange("p n t -> p (n t)").bitcast(I32))
+
+        load_rows(0, 0)
+        nc.sync.dma_start(offsets[:], offs)
+        load_rows(0, 1)
+        nc.sync.dma_start(out=limit[:], in_=lm.rearrange("(p t) o -> p (t o)", t=PACK))
+        for q in range(QUADS):
+            load_rows((2 + q) // PACK, (2 + q) % PACK)
+            load_scales(wa_sc, wa_scales, q)
+            load_scales(wb_sc, wb_scales, q)
+        load_rows(1, 2)
+        load_a(0)
+        load_rows(1, 3)
+        load_b(0)
+        load_a(1)
+        load_b(1)
+
+        nc.vector.tensor_scalar(bounded[:], limit[:], HUGE, TINY, ALU.min, ALU.max)
+        nc.vector.tensor_tensor(bound_sq[:], bounded[:], bounded[:], ALU.mult)
+        nc.scalar.activation(inv_limit[:], bound_sq[:], ACT.Abs_reciprocal_sqrt)
+        nc.vector.tensor_scalar(gain[:, :, 0], limit[:], HUGE, 1.0, ALU.min, ALU.mult)
+        nc.vector.tensor_scalar(gain[:, :, 1], limit[:], HUGE, 0.5, ALU.min, ALU.mult)
+
+        def gather(g, r):
+            nc.vector.tensor_copy(picked[g][:, :, :, r].rearrange("p t m -> p m t"), rows[g][r][:].indirect(offsets[:]))
+
+        def quantize_x(g, t0, t1):
+            cols = slice(t0 * P, t1 * P)
+            nc.vector.quantize_mx(
+                out=x_codes[g][:, cols].bitcast(FP8X4),
+                scales=x_sc[g][:, cols],
+                in_=picked[g][:, t0:t1, :, :].rearrange("p t m r -> p (t m r)"),
+            )
+
+        def multiply(g, t, which):
+            cols = slice(t * P, (t + 1) * P)
+            for acc, codes, plane in (
+                (acc_a[t], wa_codes[g][:].bitcast(FP4X4), wa_sc),
+                (acc_b[t], wb_codes[g][:].bitcast(FP8X4), wb_sc),
+            )[which]:
+                nc.tensor.matmul_mx(
+                    out=acc[:],
+                    lhsT=x_codes[g][:, cols].bitcast(FP8X4),
+                    lhsT_scale=x_sc[g][:, cols],
+                    rhs=codes,
+                    rhs_scale=plane[:, g * N : (g + 1) * N],
+                    start=(g == 0),
+                    stop=(g == PASSES - 1),
+                )
+
+        for r in range(PACK):
+            gather(0, r)
+        quantize_x(0, 0, PACK)
+        for t in range(PACK):
+            multiply(0, t, slice(0, 1))
+        for t in range(PACK):
+            multiply(0, t, slice(1, 2))
+        for r in range(PACK):
+            gather(1, r)
+        for t in range(PACK):
+            quantize_x(1, t, t + 1)
+        for t in range(PACK):
+            multiply(1, t, slice(0, 2))
+
+        root = float(N) ** -0.5
+
+        def square_a(t):
+            nc.scalar.activation(y[:, t, :], acc_a[t][:], ACT.Square, scale=root, accum_out=mean_sq[:, t, 0:1])
+
+        def square_b(t):
+            nc.scalar.activation(half_b[:, t, :], acc_b[t][:], ACT.Square, scale=root, accum_out=mean_sq[:, t, 1:2])
+
+        def stats_b(t):
+            nc.vector.bn_stats(stats[:, t, 0:6], acc_b[t][:])
+
+        def fold_b(t):
+            left = stats[:, t, 0:6].rearrange("p (h s) -> p h s", s=3)[:, :, 1:3]
+            right = stats[:, t, 1:11].rearrange("p (j s) -> p j s", s=5)[:, :, 0:4:3].rearrange("p j h -> p h j")
+            nc.vector.scalar_tensor_tensor(
+                terms[:, t, :, :], left, 0.5, right, ALU.mult, ALU.mult, accum_out=mean_sq[:, t, 1:2]
+            )
+
+        def roots(t0, t1):
+            nc.scalar.activation(inv_rms[:, t0:t1, :], mean_sq[:, t0:t1, :], ACT.Abs_reciprocal_sqrt, bias=EPS)
+
+        def factors(t):
+            nc.vector.scalar_tensor_tensor(
+                factor[:, t, :], inv_rms[:, t, :], inv_limit[:, t : t + 1], gain[:, t, :], ALU.min, ALU.mult
+            )
+
+        def scale_b_scalar(t):
+            nc.scalar.activation(half_b[:, t, :], acc_b[t][:], ACT.Copy, scale=factor[:, t, 1:2])
+
+        def scale_b_vector(t):
+            nc.vector.tensor_scalar(half_b[:, t, :], acc_b[t][:], factor[:, t, 1:2], None, ALU.mult)
+
+        def combine(t, c0, c1):
+            nc.vector.scalar_tensor_tensor(
+                y[:, t, c0:c1], acc_a[t][:, c0:c1], factor[:, t, 0:1], half_b[:, t, c0:c1], ALU.mult, ALU.add
+            )
+
+        y_rows = out_0.rearrange("(p t) n -> t p n", t=PACK)
+
+        def store_y(t):
+            nc.sync.dma_start(out=y_rows[t], in_=y[:, t, :])
+
+        def quantize_y(h):
+            cols = slice(h * HALF, (h + 1) * HALF)
+            nc.vector.quantize_mx(
+                out=y_codes[:, cols].bitcast(FP8X4), scales=y_sc[:, cols], in_=y_bf[h][:].rearrange("p n t -> p (n t)")
+            )
+            nc.sync.dma_start(
+                out=out_1[0].rearrange("p n t -> p (n t)").bitcast(I32)[:, cols], in_=y_codes[:, cols].bitcast(I32)
+            )
+
+        for t in range(PACK):
+            square_a(t)
+            if t < 3:
+                stats_b(t)
+                fold_b(t)
+            else:
+                square_b(t)
+            roots(t, t + 1)
+            factors(t)
+            if t == 0:
+                scale_b_vector(t)
+            else:
+                scale_b_scalar(t)
+            if t < 2:
+                combine(t, 0, N)
+                store_y(t)
+        combine(2, 0, HALF)
+        combine(3, 0, HALF)
+        nc.scalar.copy(y_bf[0][:], y[:, :, 0:HALF].rearrange("p t n -> p n t"))
+        combine(2, HALF, N)
+        store_y(2)
+        combine(3, HALF, N)
+        store_y(3)
+        nc.vector.tensor_copy(y_bf[1][:], y[:, :, HALF:N].rearrange("p t n -> p n t"))
+        quantize_y(0)
+        quantize_y(1)
+        for q in range(QUADS):
+            queue = nc.scalar if q % 2 else nc.sync
+            queue.dma_start(
+                out=out_2[0, 4 * q : 4 * q + 4, :].bitcast(I32), in_=y_sc[32 * q : 32 * q + 4, :].bitcast(I32)
+            )

@@ -39,7 +39,8 @@ def tile_moe_expert_rows_held_to_size_pl_kernel(tc, xt, wa_words, wa_scales, wb_
         wb_codes = [keep.tile([P, N], U32, name="wb_codes%d" % g, align_bytes=64) for g in range(PASSES)]
         wa_sc = keep.tile([P, PASSES * N], U8, name="wa_sc", align_bytes=64)
         wb_sc = keep.tile([P, PASSES * N], U8, name="wb_sc", align_bytes=64)
-        picked = [keep.tile([P, PACK, P, PACK], BF16, name="picked%d" % g, align_bytes=64) for g in range(PASSES)]
+        picked = [[keep.tile([P, 2, J], BF16, name="picked%d%d" % (g, u)) for u in range(2)] for g in range(PASSES)]
+        dealt = [[keep.tile([P, P, PACK], BF16, name="dealt%d%d" % (g, t), align_bytes=64) for t in range(PACK)] for g in range(PASSES)]
         x_codes = [keep.tile([P, J], U32, name="x_codes%d" % g, align_bytes=64) for g in range(PASSES)]
         x_sc = [keep.tile([P, J], U8, name="x_sc%d" % g, align_bytes=64) for g in range(PASSES)]
         acc_a = [psum.tile([P, N], F32, name="acc_a%d" % t) for t in range(PACK)]
@@ -87,10 +88,11 @@ def tile_moe_expert_rows_held_to_size_pl_kernel(tc, xt, wa_words, wa_scales, wb_
         for q in range(QUADS):
             load_rows((2 + q) // PACK, (2 + q) % PACK)
             load_scales(wa_sc, wa_scales, q)
-            load_scales(wb_sc, wb_scales, q)
         load_rows(1, 2)
         load_a(0)
         load_rows(1, 3)
+        for q in range(QUADS):
+            load_scales(wb_sc, wb_scales, q)
         load_b(0)
         load_a(1)
         load_b(1)
@@ -102,14 +104,17 @@ def tile_moe_expert_rows_held_to_size_pl_kernel(tc, xt, wa_words, wa_scales, wb_
         nc.vector.tensor_scalar(gain[:, :, 1], limit[:], HUGE, 0.5, ALU.min, ALU.mult)
 
         def gather(g, r):
-            nc.vector.tensor_copy(picked[g][:, :, :, r].rearrange("p t m -> p m t"), rows[g][r][:].indirect(offsets[:]))
+            nc.vector.tensor_copy(picked[g][r // 2][:, r % 2, :], rows[g][r][:].indirect(offsets[:]))
 
-        def quantize_x(g, t0, t1):
-            cols = slice(t0 * P, t1 * P)
+        def deal(copy, g, u, t):
+            copy(dealt[g][t][:, :, 2 * u : 2 * u + 2], picked[g][u][:].rearrange("p e (m t) -> p t m e", t=PACK)[:, t])
+
+        def quantize_x(g, t):
+            cols = slice(t * P, (t + 1) * P)
             nc.vector.quantize_mx(
                 out=x_codes[g][:, cols].bitcast(FP8X4),
                 scales=x_sc[g][:, cols],
-                in_=picked[g][:, t0:t1, :, :].rearrange("p t m r -> p (t m r)"),
+                in_=dealt[g][t][:].rearrange("p m r -> p (m r)"),
             )
 
         def multiply(g, t, which):
@@ -128,19 +133,24 @@ def tile_moe_expert_rows_held_to_size_pl_kernel(tc, xt, wa_words, wa_scales, wb_
                     stop=(g == PASSES - 1),
                 )
 
-        for r in range(PACK):
-            gather(0, r)
-        quantize_x(0, 0, PACK)
-        for t in range(PACK):
-            multiply(0, t, slice(0, 1))
-        for t in range(PACK):
-            multiply(0, t, slice(1, 2))
-        for r in range(PACK):
-            gather(1, r)
-        for t in range(PACK):
-            quantize_x(1, t, t + 1)
-        for t in range(PACK):
-            multiply(1, t, slice(0, 2))
+        for g in range(PASSES):
+            gather(g, 0)
+            gather(g, 1)
+            for t in range(PACK):
+                deal(nc.scalar.copy, g, 0, t)
+            gather(g, 2)
+            gather(g, 3)
+            for t in range(PACK):
+                deal(nc.vector.tensor_copy, g, 1, t)
+                quantize_x(g, t)
+            if g == 0:
+                for t in range(PACK):
+                    multiply(0, t, slice(0, 1))
+                for t in range(PACK):
+                    multiply(0, t, slice(1, 2))
+            else:
+                for t in range(PACK):
+                    multiply(1, t, slice(0, 2))
 
         root = float(N) ** -0.5
 
@@ -168,21 +178,27 @@ def tile_moe_expert_rows_held_to_size_pl_kernel(tc, xt, wa_words, wa_scales, wb_
                 factor[:, t, :], inv_rms[:, t, :], inv_limit[:, t : t + 1], gain[:, t, :], ALU.min, ALU.mult
             )
 
-        def scale_b_scalar(t):
-            nc.scalar.activation(half_b[:, t, :], acc_b[t][:], ACT.Copy, scale=factor[:, t, 1:2])
+        def scale_b_scalar(t, c0, c1):
+            nc.scalar.activation(half_b[:, t, c0:c1], acc_b[t][:, c0:c1], ACT.Copy, scale=factor[:, t, 1:2])
 
-        def scale_b_vector(t):
-            nc.vector.tensor_scalar(half_b[:, t, :], acc_b[t][:], factor[:, t, 1:2], None, ALU.mult)
+        def scale_b_vector(t, c0, c1):
+            nc.vector.tensor_scalar(half_b[:, t, c0:c1], acc_b[t][:, c0:c1], factor[:, t, 1:2], None, ALU.mult)
+
+        def round_y(copy, h, c0, c1):
+            copy(
+                y_bf[h][:, c0:c1, :].rearrange("p (c i) t -> p c t i", i=4),
+                y[:, :, h * HALF + c0 : h * HALF + c1].rearrange("p t (c i) -> p c t i", i=4),
+            )
 
         def combine(t, c0, c1):
             nc.vector.scalar_tensor_tensor(
                 y[:, t, c0:c1], acc_a[t][:, c0:c1], factor[:, t, 0:1], half_b[:, t, c0:c1], ALU.mult, ALU.add
             )
 
-        y_rows = out_0.rearrange("(p t) n -> t p n", t=PACK)
+        y_rows = out_0.rearrange("(p t) n -> p t n", t=PACK)
 
-        def store_y(t):
-            nc.sync.dma_start(out=y_rows[t], in_=y[:, t, :])
+        def store_y(c0, c1):
+            nc.sync.dma_start(out=y_rows[:, :, c0:c1], in_=y[:, :, c0:c1])
 
         def quantize_y(h):
             cols = slice(h * HALF, (h + 1) * HALF)
@@ -195,28 +211,27 @@ def tile_moe_expert_rows_held_to_size_pl_kernel(tc, xt, wa_words, wa_scales, wb_
 
         for t in range(PACK):
             square_a(t)
-            if t < 3:
+            if t == 0:
+                square_b(t)
+            else:
                 stats_b(t)
                 fold_b(t)
-            else:
-                square_b(t)
             roots(t, t + 1)
             factors(t)
-            if t == 0:
-                scale_b_vector(t)
+        for h in range(2):
+            c0, c1 = h * HALF, (h + 1) * HALF
+            for t in range(PACK):
+                if t == 1:
+                    scale_b_vector(t, c0, c1)
+                else:
+                    scale_b_scalar(t, c0, c1)
+                combine(t, c0, c1)
+            store_y(c0, c1)
+            if h == 0:
+                round_y(nc.scalar.copy, 0, 0, HALF)
             else:
-                scale_b_scalar(t)
-            if t < 2:
-                combine(t, 0, N)
-                store_y(t)
-        combine(2, 0, HALF)
-        combine(3, 0, HALF)
-        nc.scalar.copy(y_bf[0][:], y[:, :, 0:HALF].rearrange("p t n -> p n t"))
-        combine(2, HALF, N)
-        store_y(2)
-        combine(3, HALF, N)
-        store_y(3)
-        nc.vector.tensor_copy(y_bf[1][:], y[:, :, HALF:N].rearrange("p t n -> p n t"))
+                round_y(nc.scalar.copy, 1, 0, 96)
+                round_y(nc.vector.tensor_copy, 1, 96, HALF)
         quantize_y(0)
         quantize_y(1)
         for q in range(QUADS):

@@ -71,8 +71,8 @@ def tile_moe_expert_rows_held_to_size_pl_kernel(tc, xt, wa_words, wa_scales, wb_
 
         def load_scales(plane, src, q):
             nc.sync.dma_start(
-                out=plane[32 * q : 32 * q + 4, :].bitcast(I32).rearrange("r (g c) -> r g c", g=PASSES),
-                in_=src.bitcast(I32)[:, 4 * q : 4 * q + 4, :].rearrange("g r c -> r g c"),
+                out=plane[q:P:32, :].bitcast(I32).rearrange("r (g c) -> r g c", g=PASSES),
+                in_=src.bitcast(I32)[:, q:16:4, :].rearrange("g r c -> r g c"),
             )
 
         def load_a(g):
@@ -197,8 +197,8 @@ def tile_moe_expert_rows_held_to_size_pl_kernel(tc, xt, wa_words, wa_scales, wb_
 
         y_rows = out_0.rearrange("(p t) n -> p t n", t=PACK)
 
-        def store_y(c0, c1):
-            nc.sync.dma_start(out=y_rows[:, :, c0:c1], in_=y[:, :, c0:c1])
+        def store_y(t0, t1, c0, c1):
+            nc.sync.dma_start(out=y_rows[:, t0:t1, c0:c1], in_=y[:, t0:t1, c0:c1])
 
         def quantize_y(h):
             cols = slice(h * HALF, (h + 1) * HALF)
@@ -226,7 +226,10 @@ def tile_moe_expert_rows_held_to_size_pl_kernel(tc, xt, wa_words, wa_scales, wb_
                 else:
                     scale_b_scalar(t, c0, c1)
                 combine(t, c0, c1)
-            store_y(c0, c1)
+                if h == 0:
+                    store_y(t, t + 1, c0, c1)
+                elif t % 2:
+                    store_y(t - 1, t + 1, c0, c1)
             if h == 0:
                 round_y(nc.scalar.copy, 0, 0, HALF)
             else:
@@ -237,5 +240,5 @@ def tile_moe_expert_rows_held_to_size_pl_kernel(tc, xt, wa_words, wa_scales, wb_
         for q in range(QUADS):
             queue = nc.scalar if q % 2 else nc.sync
             queue.dma_start(
-                out=out_2[0, 4 * q : 4 * q + 4, :].bitcast(I32), in_=y_sc[32 * q : 32 * q + 4, :].bitcast(I32)
+                out=out_2[0, q:16:4, :].bitcast(I32), in_=y_sc[q:P:32, :].bitcast(I32)
             )

from contextlib import ExitStack

import concourse.mybir as mybir

K, T, J, N = 1024, 2048, 512, 512
FLOPS = 2 * 2 * J * K * N

F32 = mybir.dt.float32
BF16 = mybir.dt.bfloat16
I32 = mybir.dt.int32
U32 = mybir.dt.uint32
U16 = mybir.dt.uint16
U8 = mybir.dt.uint8
FP8X4 = mybir.dt.float8_e4m3fn_x4
FP4X4 = mybir.dt.float4_e2m1fn_x4
ALU = mybir.AluOpType
ACT = mybir.ActivationFunctionType

P = 128
PACK = 4
PASSES = K // (P * PACK)
QUADS = 4
EPS = 0.01
TINY = 1e-15
HUGE = 1e15
HALF = N // 2


def tile_moe_expert_rows_held_to_size_pl_kernel(tc, xt, wa_words, wa_scales, wb_words, wb_scales, lm, offs, out_0, out_1, out_2):
    nc = tc.nc
    with ExitStack() as ctx:
        keep = ctx.enter_context(tc.tile_pool(name="keep", bufs=1))
        psum = ctx.enter_context(tc.psum_pool(name="psum", bufs=1))

        offsets = keep.tile([P, J // 16], U16, name="offsets")
        limit = keep.tile([P, PACK], F32, name="limit")
        rows = [[keep.tile([P, T], F32, name="rows%d%d" % (g, r)) for r in range(PACK)] for g in range(PASSES)]
        wa_codes = [keep.tile([P, 2 * N], U8, name="wa_codes%d" % g, align_bytes=64) for g in range(PASSES)]
        wb_codes = [keep.tile([P, N], U32, name="wb_codes%d" % g, align_bytes=64) for g in range(PASSES)]
        wa_sc = keep.tile([P, PASSES * N], U8, name="wa_sc", align_bytes=64)
        wb_sc = keep.tile([P, PASSES * N], U8, name="wb_sc", align_bytes=64)
        picked = [[keep.tile([P, 2, J], BF16, name="picked%d%d" % (g, u)) for u in range(2)] for g in range(PASSES)]
        dealt = [[keep.tile([P, P, PACK], BF16, name="dealt%d%d" % (g, t), align_bytes=64) for t in range(PACK)] for g in range(PASSES)]
        x_codes = [keep.tile([P, J], U32, name="x_codes%d" % g, align_bytes=64) for g in range(PASSES)]
        x_sc = [keep.tile([P, J], U8, name="x_sc%d" % g, align_bytes=64) for g in range(PASSES)]
        acc_a = [psum.tile([P, N], F32, name="acc_a%d" % t) for t in range(PACK)]
        acc_b = [psum.tile([P, N], F32, name="acc_b%d" % t) for t in range(PACK)]
        y = keep.tile([P, PACK, N], F32, name="y")
        half_b = keep.tile([P, PACK, N], F32, name="half_b")
        y_bf = [keep.tile([P, HALF, PACK], BF16, name="y_bf%d" % h, align_bytes=64) for h in range(2)]
        y_codes = keep.tile([P, N], U32, name="y_codes", align_bytes=64)
        y_sc = keep.tile([P, N], U8, name="y_sc", align_bytes=64)
        mean_sq = keep.tile([P, PACK, 2], F32, name="mean_sq")
        inv_rms = keep.tile([P, PACK, 2], F32, name="inv_rms")
        factor = keep.tile([P, PACK, 2], F32, name="factor")
        gain = keep.tile([P, PACK, 2], F32, name="gain")
        bound_sq = keep.tile([P, PACK], F32, name="bound_sq")
        bounded = keep.tile([P, PACK], F32, name="bounded")
        inv_limit = keep.tile([P, PACK], F32, name="inv_limit")
        stats = keep.tile([P, PACK, 16], F32, name="stats")
        terms = keep.tile([P, PACK, 2, 2], F32, name="terms")
        nc.vector.memset(stats[:, :, 6:10], 2.0 / N)

        nc.vector.memset(wa_sc[:].bitcast(I32), 0)
        nc.vector.memset(wb_sc[:].bitcast(I32), 0)

        x_rows = xt.rearrange("(g p r) t -> g r p t", p=P, r=PACK)

        def load_rows(g, r):
            nc.sync.dma_start(out=rows[g][r][:], in_=x_rows[g, r])

        def load_scales(plane, src, q):
            nc.sync.dma_start(
                out=plane[q:P:32, :].bitcast(I32).rearrange("r (g c) -> r g c", g=PASSES),
                in_=src.bitcast(I32)[:, q:16:4, :].rearrange("g r c -> r g c"),
            )

        def load_a(g):
            nc.sync.dma_start(out=wa_codes[g][:].bitcast(I32), in_=wa_words[g].bitcast(I32))

        def load_b(g):
            nc.sync.dma_start(out=wb_codes[g][:].bitcast(I32), in_=wb_words[g].rearrange("p n t -> p (n t)").bitcast(I32))

        load_rows(0, 0)
        nc.sync.dma_start(offsets[:], offs)
        load_rows(0, 1)
        nc.sync.dma_start(out=limit[:], in_=lm.rearrange("(p t) o -> p (t o)", t=PACK))
        for q in range(QUADS):
            load_rows((2 + q) // PACK, (2 + q) % PACK)
            load_scales(wa_sc, wa_scales, q)
        load_rows(1, 2)
        load_a(0)
        load_rows(1, 3)
        for q in range(QUADS):
            load_scales(wb_sc, wb_scales, q)
        load_b(0)
        load_a(1)
        load_b(1)

        nc.vector.tensor_scalar(bounded[:], limit[:], HUGE, TINY, ALU.min, ALU.max)
        nc.vector.tensor_tensor(bound_sq[:], bounded[:], bounded[:], ALU.mult)
        nc.scalar.activation(inv_limit[:], bound_sq[:], ACT.Abs_reciprocal_sqrt)
        nc.vector.tensor_scalar(gain[:, :, 0], limit[:], HUGE, 1.0, ALU.min, ALU.mult)
        nc.vector.tensor_scalar(gain[:, :, 1], limit[:], HUGE, 0.5, ALU.min, ALU.mult)

        def gather(g, r):
            nc.vector.tensor_copy(picked[g][r // 2][:, r % 2, :], rows[g][r][:].indirect(offsets[:]))

        def deal(copy, g, u, t):
            copy(dealt[g][t][:, :, 2 * u : 2 * u + 2], picked[g][u][:].rearrange("p e (m t) -> p t m e", t=PACK)[:, t])

        def quantize_x(g, t):
            cols = slice(t * P, (t + 1) * P)
            nc.vector.quantize_mx(
                out=x_codes[g][:, cols].bitcast(FP8X4),
                scales=x_sc[g][:, cols],
                in_=dealt[g][t][:].rearrange("p m r -> p (m r)"),
            )

        def multiply(g, t, which):
            cols = slice(t * P, (t + 1) * P)
            for acc, codes, plane in (
                (acc_a[t], wa_codes[g][:].bitcast(FP4X4), wa_sc),
                (acc_b[t], wb_codes[g][:].bitcast(FP8X4), wb_sc),
            )[which]:
                nc.tensor.matmul_mx(
                    out=acc[:],
                    lhsT=x_codes[g][:, cols].bitcast(FP8X4),
                    lhsT_scale=x_sc[g][:, cols],
                    rhs=codes,
                    rhs_scale=plane[:, g * N : (g + 1) * N],
                    start=(g == 0),
                    stop=(g == PASSES - 1),
                )

        for g in range(PASSES):
            gather(g, 0)
            gather(g, 1)
            for t in range(PACK):
                deal(nc.scalar.copy, g, 0, t)
            gather(g, 2)
            gather(g, 3)
            for t in range(PACK):
                deal(nc.vector.tensor_copy, g, 1, t)
                quantize_x(g, t)
            if g == 0:
                for t in range(PACK):
                    multiply(0, t, slice(0, 1))
                for t in range(PACK):
                    multiply(0, t, slice(1, 2))
            else:
                for t in range(PACK):
                    multiply(1, t, slice(0, 2))

        root = float(N) ** -0.5

        def square_a(t):
            nc.scalar.activation(y[:, t, :], acc_a[t][:], ACT.Square, scale=root, accum_out=mean_sq[:, t, 0:1])

        def square_b(t):
            nc.scalar.activation(half_b[:, t, :], acc_b[t][:], ACT.Square, scale=root, accum_out=mean_sq[:, t, 1:2])

        def stats_b(t):
            nc.vector.bn_stats(stats[:, t, 0:6], acc_b[t][:])

        def fold_b(t):
            left = stats[:, t, 0:6].rearrange("p (h s) -> p h s", s=3)[:, :, 1:3]
            right = stats[:, t, 1:11].rearrange("p (j s) -> p j s", s=5)[:, :, 0:4:3].rearrange("p j h -> p h j")
            nc.vector.scalar_tensor_tensor(
                terms[:, t, :, :], left, 0.5, right, ALU.mult, ALU.mult, accum_out=mean_sq[:, t, 1:2]
            )

        def roots(t0, t1):
            nc.scalar.activation(inv_rms[:, t0:t1, :], mean_sq[:, t0:t1, :], ACT.Abs_reciprocal_sqrt, bias=EPS)

        def factors(t):
            nc.vector.scalar_tensor_tensor(
                factor[:, t, :], inv_rms[:, t, :], inv_limit[:, t : t + 1], gain[:, t, :], ALU.min, ALU.mult
            )

        def scale_b_scalar(t, c0, c1):
            nc.scalar.activation(half_b[:, t, c0:c1], acc_b[t][:, c0:c1], ACT.Copy, scale=factor[:, t, 1:2])

        def scale_b_vector(t, c0, c1):
            nc.vector.tensor_scalar(half_b[:, t, c0:c1], acc_b[t][:, c0:c1], factor[:, t, 1:2], None, ALU.mult)

        def round_y(copy, h, c0, c1):
            copy(
                y_bf[h][:, c0:c1, :].rearrange("p (c i) t -> p c t i", i=4),
                y[:, :, h * HALF + c0 : h * HALF + c1].rearrange("p t (c i) -> p c t i", i=4),
            )

        def combine(t, c0, c1):
            nc.vector.scalar_tensor_tensor(
                y[:, t, c0:c1], acc_a[t][:, c0:c1], factor[:, t, 0:1], half_b[:, t, c0:c1], ALU.mult, ALU.add
            )

        y_rows = out_0.rearrange("(p t) n -> p t n", t=PACK)

        def store_y(t0, t1, c0, c1):
            nc.sync.dma_start(out=y_rows[:, t0:t1, c0:c1], in_=y[:, t0:t1, c0:c1])

        def quantize_y(h):
            cols = slice(h * HALF, (h + 1) * HALF)
            nc.vector.quantize_mx(
                out=y_codes[:, cols].bitcast(FP8X4), scales=y_sc[:, cols], in_=y_bf[h][:].rearrange("p n t -> p (n t)")
            )
            nc.sync.dma_start(
                out=out_1[0].rearrange("p n t -> p (n t)").bitcast(I32)[:, cols], in_=y_codes[:, cols].bitcast(I32)
            )

        for t in range(PACK):
            square_a(t)
            if t == 0:
                square_b(t)
            else:
                stats_b(t)
                fold_b(t)
            roots(t, t + 1)
            factors(t)
        for h in range(2):
            c0, c1 = h * HALF, (h + 1) * HALF
            for t in range(PACK):
                if t == 1:
                    scale_b_vector(t, c0, c1)
                else:
                    scale_b_scalar(t, c0, c1)
                combine(t, c0, c1)
                if h == 0:
                    store_y(t, t + 1, c0, c1)
                elif t % 2:
                    store_y(t - 1, t + 1, c0, c1)
            if h == 0:
                round_y(nc.scalar.copy, 0, 0, HALF)
            else:
                round_y(nc.scalar.copy, 1, 0, 96)
                round_y(nc.vector.tensor_copy, 1, 96, HALF)
        quantize_y(0)
        quantize_y(1)
        for q in range(QUADS):
            queue = nc.scalar if q % 2 else nc.sync
            queue.dma_start(
                out=out_2[0, q:16:4, :].bitcast(I32), in_=y_sc[q:P:32, :].bitcast(I32)
            )
